import numpy as np
import ml_dtypes


def mxq(x, axis, fmt="e4m3"):
    dtype, down = {"e4m3": (ml_dtypes.float8_e4m3fn, 7), "e5m2": (ml_dtypes.float8_e5m2, 14)}[fmt]
    v = np.moveaxis(np.asarray(x, np.float32).astype(ml_dtypes.bfloat16).astype(np.float64), axis, -1)
    blocks = v.reshape(v.shape[:-1] + (-1, 32))
    amax = np.abs(blocks).max(-1, keepdims=True)
    byte = np.maximum(np.where(amax > 0, np.frexp(amax)[1] - 1 + 127, 0) - down, 1)
    scale = np.exp2(byte - 127.0)
    codes = (blocks / scale).astype(np.float32).astype(dtype).astype(np.float64)
    return np.moveaxis((codes * scale).reshape(v.shape), -1, axis)


WIDE = False


def mx_kscale(k):
    if not WIDE:
        return np.ones(k)
    levels = np.array([30, -30])
    if k % 512:
        return np.exp2(np.random.permutation(np.resize(levels, k // 32))).repeat(32)
    a = np.empty((k // 512, 16))
    for p in range(k // 512):
        a[p, :8] = np.random.permutation(np.resize(levels, 8))
        for g in range(8):
            far = levels[np.abs(levels - a[p, g]) >= 10]
            a[p, g + 8] = far[np.random.randint(len(far))]
    return np.exp2(a.ravel()).repeat(32)


def f64(x):
    return np.asarray(x).astype(np.float64)


def striped(idx):
    return np.tile(np.asarray(idx).reshape(-1, 16).T, (8, 1)).astype(np.uint16)


def unstriped(offs):
    return offs[:16].T.reshape(-1).astype(np.int64)


E2M1 = np.array([0.0, 0.5, 1.0, 1.5, 2.0, 3.0, 4.0, 6.0, -0.0, -0.5, -1.0, -1.5, -2.0, -3.0, -4.0, -6.0])


def pack_weight(w, fmt):
    k, n = w.shape
    w = f64(np.asarray(w, np.float32).astype(ml_dtypes.bfloat16)).reshape(k // 32, 32, n)
    amax = np.abs(w).max(1)
    if fmt in ("e4m3", "e5m2"):
        byte = np.frexp(amax)[1] - 1 + 127 - (7 if fmt == "e4m3" else 14)
    else:
        mant, ex = np.frexp(amax / 6.0)
        byte = np.where(mant > 0.5, ex, ex - 1) + 127
    byte = np.clip(np.where(amax > 0, byte, 1), 1, 254)
    scaled = (w * np.exp2(127.0 - byte)[:, None, :]).reshape(k, n).astype(np.float32)
    by_word = np.ascontiguousarray(scaled.reshape(k // 512, 128, 4, n).transpose(0, 1, 3, 2))
    if fmt in ("e4m3", "e5m2"):
        words = by_word.astype(ml_dtypes.float8_e4m3fn if fmt == "e4m3" else ml_dtypes.float8_e5m2).view(np.uint8)
    else:
        c = by_word.astype(ml_dtypes.float4_e2m1fn).view(np.uint8) & 0xF
        words = (c[..., 0::2] | (c[..., 1::2] << 4)).reshape(k // 512, 128, 2 * n)
    return np.ascontiguousarray(words), np.ascontiguousarray(byte.astype(np.uint8).reshape(k // 512, 16, n))


def unpack_weight(words, scales, fmt):
    g, _, n = scales.shape
    words = np.ascontiguousarray(words).reshape(g, 128, n, -1)
    if fmt in ("e4m3", "e5m2"):
        vals = words.view(ml_dtypes.float8_e4m3fn if fmt == "e4m3" else ml_dtypes.float8_e5m2).astype(np.float64)
    else:
        nib = np.empty((g, 128, n, 4), np.uint8)
        nib[..., 0::2] = words & 0xF
        nib[..., 1::2] = words >> 4
        vals = E2M1[nib]
    vals = vals * np.repeat(np.exp2(scales.astype(np.float64) - 127.0), 8, axis=1)[..., None]
    return vals.transpose(0, 1, 3, 2).reshape(g * 512, n)


def sigmoid(v):
    return 1.0 / (1.0 + np.exp(-v))


K, T, Z, J, R, O, N, E = 512, 1024, 1024, 256, 512, 256, 256, 1024


def setup_inputs():
    n = np.random.standard_normal
    idx = np.random.permutation(T)[:J]
    idx2 = np.random.permutation(Z)[:J]
    idx3 = np.random.permutation(J)[:O]
    idx4 = np.random.permutation(O)[:O]
    idx5 = np.random.permutation(J)[:O]
    idx6 = np.random.permutation(T)[:O]
    idx7 = np.random.permutation(E)[:O]
    fk = mx_kscale(K)
    fr = mx_kscale(R)
    xtp = pack_weight(n((K, T)) / fk[:, None], "e5m2")
    xop = pack_weight(n((K, Z)) / fk[:, None], "e4m3")
    wp = pack_weight(n((K, R)) * 1 / np.sqrt(K) * fk[:, None] * fr, "e2m1")
    wbp = pack_weight(n((R, N)) * 1 / np.sqrt(R) / fr[:, None], "e2m1")
    wsp = pack_weight(n((K, N)) * 1 / np.sqrt(K) * fk[:, None], "e2m1")
    return {
        "xt_words": xtp[0],
        "xt_scales": xtp[1],
        "xo_words": xop[0],
        "xo_scales": xop[1],
        "w_words": wp[0],
        "w_scales": wp[1],
        "wb_words": wbp[0],
        "wb_scales": wbp[1],
        "ws_words": wsp[0],
        "ws_scales": wsp[1],
        "tz": (n((N, E))).astype(np.float32),
        "so": (np.random.uniform(0.6, 1.6, (N, 1))).astype(np.float32),
        "bo": (np.random.uniform(-1.0, 1.0, (N, 1))).astype(np.float32),
        "offs": striped(idx),
        "offs2": striped(idx2),
        "offs3": striped(idx3),
        "offs4": striped(idx4),
        "offs5": striped(idx5),
        "offs6": striped(idx6),
        "offs7": striped(idx7),
    }


def reference(xt_words, xt_scales, xo_words, xo_scales, w_words, w_scales, wb_words, wb_scales, ws_words, ws_scales, tz, so, bo, offs, offs2, offs3, offs4, offs5, offs6, offs7):
    idx = unstriped(offs)
    idx2 = unstriped(offs2)
    idx3 = unstriped(offs3)
    idx4 = unstriped(offs4)
    idx5 = unstriped(offs5)
    idx6 = unstriped(offs6)
    idx7 = unstriped(offs7)
    xtu = unpack_weight(xt_words, xt_scales, "e5m2")
    xou = unpack_weight(xo_words, xo_scales, "e4m3")
    wu = unpack_weight(w_words, w_scales, "e2m1")
    wbu = unpack_weight(wb_words, wb_scales, "e2m1")
    wsu = unpack_weight(ws_words, ws_scales, "e2m1")
    xtidxg = xtu[:, idx]
    a = wu.T @ xtidxg
    xoidx2g = xou[:, idx2]
    b = wu.T @ xoidx2g
    ca = a[:, idx3]
    hid = np.abs(ca[:, idx4] - b[:, idx5])
    hidq = mxq(hid, 0, "e4m3")
    xtidx6g = xtu[:, idx6]
    p = wbu.T @ hidq + wsu.T @ xtidx6g
    y = p * sigmoid(f64(tz)[:, idx7] * f64(so) + f64(bo))
    return y

@@ -1,0 +1,223 @@
+from contextlib import ExitStack
+
+import concourse.mybir as mybir
+
+F32 = mybir.dt.float32
+BF16 = mybir.dt.bfloat16
+I32 = mybir.dt.int32
+U32 = mybir.dt.uint32
+U16 = mybir.dt.uint16
+U8 = mybir.dt.uint8
+E4M3 = mybir.dt.float8_e4m3fn_x4
+E5M2 = mybir.dt.float8_e5m2_x4
+E2M1 = mybir.dt.float4_e2m1fn_x4
+ACT = mybir.ActivationFunctionType
+ALU = mybir.AluOpType
+
+P = 128
+PACK = 4
+K, T, J, R, O, N, E = 512, 1024, 256, 512, 256, 256, 1024
+HALF = O // 2
+LIST_COLS = J // 16
+HALF_COLS = LIST_COLS // 2
+
+FLOPS = 2 * (2 * K * R * J + R * N * O + K * N * O)
+
+
+def tile_list_secondhand_oneforboth_further_finalgate_kernel(
+    tc, xt_words, xt_scales, xo_words, xo_scales, w_words, w_scales, wb_words, wb_scales, ws_words, ws_scales,
+    tz, so, bo, offs, offs2, offs3, offs4, offs5, offs6, offs7, out,
+):
+    nc = tc.nc
+    with ExitStack() as ctx:
+        keep = ctx.enter_context(tc.tile_pool(name="keep", bufs=1))
+        psum = ctx.enter_context(tc.psum_pool(name="psum", bufs=1))
+
+        def load_list(src, name):
+            lst = keep.tile([P, LIST_COLS], U16, name=name)
+            nc.sync.dma_start(lst[:], src)
+            return lst
+
+        def load_fp8_words(queue, src, name):
+            words = keep.tile([P, T], U32, name=name, align_bytes=64)
+            queue.dma_start(words[:].bitcast(I32), src[0].rearrange("p c t -> p (c t)").bitcast(I32))
+            return words
+
+        def load_fp4_words(queue, src, name):
+            words = keep.tile([P, src.shape[2]], U8, name=name, align_bytes=64)
+            queue.dma_start(words[:].bitcast(I32), src[0].bitcast(I32))
+            return words
+
+        def load_plane(queues, src, name):
+            width = src.shape[2]
+            plane = keep.tile([P, width], U8, name=name, align_bytes=64)
+            rows = src[0].bitcast(I32)
+            for q in range(4):
+                four = rows[4 * q : 4 * q + 4, :].unsqueeze(0).to_broadcast([8, 4, width // 4])
+                queues[q].dma_start(plane[32 * q : 32 * q + 32, :].bitcast(I32), four)
+            return plane
+
+        def load_columns(src, name):
+            cols = keep.tile([P, 2], F32, name=name)
+            with nc.allow_non_contiguous_dma(reason="one value a partition"):
+                nc.gpsimd.dma_start(cols[:], src.rearrange("(h p) o -> p (h o)", p=P))
+            return cols
+
+        def load_gate_rows(h):
+            rows = keep.tile([P, E], F32, name="tz%d" % h, tag="tz%d" % h)
+            nc.sync.dma_start(rows[:], tz[h * P : (h + 1) * P, :])
+            return rows
+
+        on_sync = [nc.sync] * 4
+        xt_w = load_fp8_words(nc.scalar, xt_words, "xt_w")
+        l1 = load_list(offs, "l1")
+        xt_s = load_plane(on_sync, xt_scales, "xt_s")
+        w_w = load_fp4_words(nc.sync, w_words, "w_w")
+        w_s = load_plane([nc.sync, nc.sync, nc.gpsimd, nc.gpsimd], w_scales, "w_s")
+        tz0 = load_gate_rows(0)
+        l7 = load_list(offs7, "l7")
+        l6 = load_list(offs6, "l6")
+        slope = load_columns(so, "slope")
+        offset = load_columns(bo, "offset")
+        xo_w = load_fp8_words(nc.sync, xo_words, "xo_w")
+        l2 = load_list(offs2, "l2")
+        xo_s = load_plane(on_sync, xo_scales, "xo_s")
+        l3 = load_list(offs3, "l3")
+        l5 = load_list(offs5, "l5")
+        l4 = load_list(offs4, "l4")
+        tz1 = load_gate_rows(1)
+        ws_w = load_fp4_words(nc.sync, ws_words, "ws_w")
+        ws_s = load_plane(on_sync, ws_scales, "ws_s")
+        wb_w = load_fp4_words(nc.sync, wb_words, "wb_w")
+        wb_s = load_plane([nc.gpsimd] * 4, wb_scales, "wb_s")
+
+        wp_w = keep.tile([P, 2 * R], U8, name="wp_w", align_bytes=64)
+        wp_s = keep.tile([P, R], U8, name="wp_s", align_bytes=64)
+        nc.vector.tensor_copy(
+            out=wp_w[:].bitcast(U16).rearrange("p (t m) -> p t m", t=PACK),
+            in_=w_w[:].bitcast(U16).rearrange("p (m t) -> p t m", t=PACK),
+        )
+        nc.vector.tensor_copy(
+            out=wp_s[:].rearrange("p (t m) -> p t m", t=PACK),
+            in_=w_s[:].rearrange("p (m t) -> p t m", t=PACK),
+        )
+
+        def gather_packed(words, plane, lst, name):
+            got_w = keep.tile([P, J], U32, name=name + "_w", align_bytes=64)
+            got_s = keep.tile([P, J], U8, name=name + "_s", align_bytes=64)
+            nc.vector.tensor_copy(out=got_w[:], in_=words[:].indirect(lst[:]))
+            nc.vector.tensor_copy(out=got_s[:], in_=plane[:].indirect(lst[:]))
+            return got_w, got_s
+
+        def first_stage(got_w, got_s, fmt, name, evacuate):
+            res = []
+            for t in range(PACK):
+                acc = psum.tile([P, J], F32, name="acc_%s%d" % (name, t), tag="bank_%s%d" % (name, t))
+                nc.tensor.matmul_mx(
+                    out=acc[:],
+                    lhsT=wp_w[:, 2 * P * t : 2 * P * (t + 1)].bitcast(E2M1),
+                    lhsT_scale=wp_s[:, P * t : P * (t + 1)],
+                    rhs=got_w[:].bitcast(fmt),
+                    rhs_scale=got_s[:],
+                    start=True,
+                    stop=True,
+                )
+                rows = keep.tile([P, J], F32, name="%s%d" % (name, t))
+                evacuate(out=rows[:], in_=acc[:])
+                res.append(rows)
+            return res
+
+        def half_list(lst, h):
+            return lst[:, h * HALF_COLS : (h + 1) * HALF_COLS]
+
+        def half(h):
+            return slice(h * HALF, (h + 1) * HALF)
+
+        def scalar_gather(dst, window):
+            nc.scalar.activation(out=dst, in_=window, func=ACT.Copy)
+
+        def vector_gather(dst, window):
+            nc.vector.tensor_copy(out=dst, in_=window)
+
+        gate = keep.tile([P, 2, O], F32, name="gate")
+
+        def gate_rows(rows, h):
+            nc.scalar.activation(
+                out=gate[:, h, :], in_=rows[:].indirect(l7[:]), func=ACT.Sigmoid,
+                bias=offset[:, h : h + 1], scale=slope[:, h : h + 1],
+            )
+
+        xa_w, xa_s = gather_packed(xt_w, xt_s, l1, "xa")
+        gate_rows(tz0, 0)
+        a = first_stage(xa_w, xa_s, E5M2, "a", nc.scalar.copy)
+        xs_w, xs_s = gather_packed(xt_w, xt_s, l6, "xs")
+        xb_w, xb_s = gather_packed(xo_w, xo_s, l2, "xb")
+
+        ca = []
+        for t in range(PACK):
+            if t == 0:
+                picked = keep.tile([P, O], F32, name="ca0", tag="tz0")
+            else:
+                picked = keep.tile([P, O], F32, name="ca%d" % t)
+            for h in range(2):
+                scalar_gather(picked[:, half(h)], a[t][:].indirect(half_list(l3, h)))
+            ca.append(picked)
+
+        b = first_stage(xb_w, xb_s, E4M3, "b", nc.vector.tensor_copy)
+
+        sums = []
+        for h in range(2):
+            acc = psum.tile([P, 2, HALF], F32, name="sum%d" % h, tag="bank_a%d" % h)
+            for g in range(2):
+                nc.tensor.matmul_mx(
+                    out=acc[:, g, :],
+                    lhsT=ws_w[:, 2 * P * g : 2 * P * (g + 1)].bitcast(E2M1),
+                    lhsT_scale=ws_s[:, P * g : P * (g + 1)],
+                    rhs=xs_w[:, half(h)].bitcast(E5M2),
+                    rhs_scale=xs_s[:, half(h)],
+                    start=(g == 0),
+                    stop=False,
+                )
+            sums.append(acc)
+
+        bg = [[keep.tile([P, HALF], F32, name="bg%d_%d" % (h, t)) for t in range(PACK)] for h in range(2)]
+        for h in range(2):
+            for t in range(PACK):
+                gather = vector_gather if t < 2 else scalar_gather
+                gather(bg[h][t][:], b[t][:].indirect(half_list(l5, h)))
+
+        diff = [keep.tile([P, PACK, HALF], F32, name="diff%d" % h) for h in range(2)]
+        for h in range(2):
+            for t in range(PACK):
+                nc.vector.tensor_tensor(
+                    out=diff[h][:, t, :], in0=ca[t][:].indirect(half_list(l4, h)), in1=bg[h][t][:], op=ALU.subtract
+                )
+        gate_rows(tz1, 1)
+
+        out_view = out.rearrange("(g p) o -> p g o", p=P)
+        hid = []
+        for h in range(2):
+            rounded = keep.tile([P, HALF * PACK], BF16, name="hid%d" % h, align_bytes=64)
+            nc.scalar.activation(
+                out=rounded[:].rearrange("p (c i t) -> p c t i", i=4, t=PACK),
+                in_=diff[h][:].rearrange("p t (c i) -> p c t i", i=4),
+                func=ACT.Abs,
+            )
+            hid.append(rounded)
+        for h in range(2):
+            hq_w = keep.tile([P, HALF], U32, name="hq_w%d" % h, align_bytes=64)
+            hq_s = keep.tile([P, HALF], U8, name="hq_s%d" % h, align_bytes=64)
+            nc.vector.quantize_mx(out=hq_w[:].bitcast(E4M3), scales=hq_s[:], in_=hid[h][:])
+            for g in range(2):
+                nc.tensor.matmul_mx(
+                    out=sums[h][:, g, :],
+                    lhsT=wb_w[:, 2 * P * g : 2 * P * (g + 1)].bitcast(E2M1),
+                    lhsT_scale=wb_s[:, P * g : P * (g + 1)],
+                    rhs=hq_w[:].bitcast(E4M3),
+                    rhs_scale=hq_s[:],
+                    start=False,
+                    stop=(g == 1),
+                )
+            y = keep.tile([P, 2, HALF], F32, name="y%d" % h)
+            nc.vector.tensor_tensor(out=y[:], in0=sums[h][:], in1=gate[:, :, half(h)], op=ALU.mult)
+            nc.sync.dma_start(out_view[:, :, half(h)], y[:])

@@ -48,48 +48,52 @@ def tile_list_secondhand_oneforboth_further_finalgate_kernel(
             queue.dma_start(words[:].bitcast(I32), src[0].bitcast(I32))
             return words
 
-        def load_plane(queues, src, name):
-            width = src.shape[2]
-            plane = keep.tile([P, width], U8, name=name, align_bytes=64)
+        def new_plane(src, name):
+            return keep.tile([P, src.shape[2]], U8, name=name, tag=name, align_bytes=64)
+
+        def load_quadrants(plane, src, quadrants):
             rows = src[0].bitcast(I32)
-            for q in range(4):
-                four = rows[4 * q : 4 * q + 4, :].unsqueeze(0).to_broadcast([8, 4, width // 4])
-                queues[q].dma_start(plane[32 * q : 32 * q + 32, :].bitcast(I32), four)
-            return plane
+            for q in quadrants:
+                four = rows[4 * q : 4 * q + 4, :].unsqueeze(0).to_broadcast([8, 4, rows.shape[1]])
+                nc.sync.dma_start(plane[32 * q : 32 * q + 32, :].bitcast(I32), four)
 
         def load_columns(src, name):
             cols = keep.tile([P, 2], F32, name=name)
             with nc.allow_non_contiguous_dma(reason="one value a partition"):
-                nc.gpsimd.dma_start(cols[:], src.rearrange("(h p) o -> p (h o)", p=P))
+                nc.sync.dma_start(cols[:], src.rearrange("(h p) o -> p (h o)", p=P))
             return cols
 
         def load_gate_rows(h):
-            rows = keep.tile([P, E], F32, name="tz%d" % h, tag="tz%d" % h)
+            rows = keep.tile([P, E], F32, name="tz%d" % h)
             nc.sync.dma_start(rows[:], tz[h * P : (h + 1) * P, :])
             return rows
 
-        on_sync = [nc.sync] * 4
-        xt_w = load_fp8_words(nc.scalar, xt_words, "xt_w")
         l1 = load_list(offs, "l1")
-        xt_s = load_plane(on_sync, xt_scales, "xt_s")
-        w_w = load_fp4_words(nc.sync, w_words, "w_w")
-        w_s = load_plane([nc.sync, nc.sync, nc.gpsimd, nc.gpsimd], w_scales, "w_s")
-        tz0 = load_gate_rows(0)
-        l7 = load_list(offs7, "l7")
         l6 = load_list(offs6, "l6")
-        slope = load_columns(so, "slope")
-        offset = load_columns(bo, "offset")
+        xt_s = new_plane(xt_scales, "xt_s")
+        load_quadrants(xt_s, xt_scales, range(4))
+        w_w = load_fp4_words(nc.sync, w_words, "w_w")
+        xt_w = load_fp8_words(nc.sync, xt_words, "xt_w")
+        w_s = new_plane(w_scales, "w_s")
+        load_quadrants(w_s, w_scales, range(4))
         xo_w = load_fp8_words(nc.sync, xo_words, "xo_w")
         l2 = load_list(offs2, "l2")
-        xo_s = load_plane(on_sync, xo_scales, "xo_s")
+        xo_s = new_plane(xo_scales, "xo_s")
+        load_quadrants(xo_s, xo_scales, range(4))
         l3 = load_list(offs3, "l3")
         l5 = load_list(offs5, "l5")
         l4 = load_list(offs4, "l4")
+        l7 = load_list(offs7, "l7")
+        tz0 = load_gate_rows(0)
         tz1 = load_gate_rows(1)
+        slope = load_columns(so, "slope")
+        offset = load_columns(bo, "offset")
         ws_w = load_fp4_words(nc.sync, ws_words, "ws_w")
-        ws_s = load_plane(on_sync, ws_scales, "ws_s")
+        ws_s = new_plane(ws_scales, "ws_s")
+        load_quadrants(ws_s, ws_scales, range(4))
         wb_w = load_fp4_words(nc.sync, wb_words, "wb_w")
-        wb_s = load_plane([nc.gpsimd] * 4, wb_scales, "wb_s")
+        wb_s = new_plane(wb_scales, "wb_s")
+        load_quadrants(wb_s, wb_scales, range(4))
 
         wp_w = keep.tile([P, 2 * R], U8, name="wp_w", align_bytes=64)
         wp_s = keep.tile([P, R], U8, name="wp_s", align_bytes=64)
@@ -102,11 +106,11 @@ def tile_list_secondhand_oneforboth_further_finalgate_kernel(
             in_=w_s[:].rearrange("p (m t) -> p t m", t=PACK),
         )
 
-        def gather_packed(words, plane, lst, name):
-            got_w = keep.tile([P, J], U32, name=name + "_w", align_bytes=64)
+        def gather_packed(words, plane, lst, name, words_tag):
+            got_w = keep.tile([P, J], U32, name=name + "_w", tag=words_tag, align_bytes=64)
             got_s = keep.tile([P, J], U8, name=name + "_s", align_bytes=64)
-            nc.vector.tensor_copy(out=got_w[:], in_=words[:].indirect(lst[:]))
             nc.vector.tensor_copy(out=got_s[:], in_=plane[:].indirect(lst[:]))
+            nc.vector.tensor_copy(out=got_w[:], in_=words[:].indirect(lst[:]))
             return got_w, got_s
 
         def first_stage(got_w, got_s, fmt, name, evacuate):
@@ -122,7 +126,7 @@ def tile_list_secondhand_oneforboth_further_finalgate_kernel(
                     start=True,
                     stop=True,
                 )
-                rows = keep.tile([P, J], F32, name="%s%d" % (name, t))
+                rows = keep.tile([P, J], F32, name="%s%d" % (name, t), tag="%s%d" % (name, t))
                 evacuate(out=rows[:], in_=acc[:])
                 res.append(rows)
             return res
@@ -139,31 +143,24 @@ def tile_list_secondhand_oneforboth_further_finalgate_kernel(
         def vector_gather(dst, window):
             nc.vector.tensor_copy(out=dst, in_=window)
 
-        gate = keep.tile([P, 2, O], F32, name="gate")
-
-        def gate_rows(rows, h):
+        def gate_rows(gate, rows, h):
             nc.scalar.activation(
                 out=gate[:, h, :], in_=rows[:].indirect(l7[:]), func=ACT.Sigmoid,
                 bias=offset[:, h : h + 1], scale=slope[:, h : h + 1],
             )
 
-        xa_w, xa_s = gather_packed(xt_w, xt_s, l1, "xa")
-        gate_rows(tz0, 0)
+        xa_w, xa_s = gather_packed(xt_w, xt_s, l1, "xa", "xa_w")
         a = first_stage(xa_w, xa_s, E5M2, "a", nc.scalar.copy)
-        xs_w, xs_s = gather_packed(xt_w, xt_s, l6, "xs")
-        xb_w, xb_s = gather_packed(xo_w, xo_s, l2, "xb")
+        xs_w, xs_s = gather_packed(xt_w, xt_s, l6, "xs", "w_s")
+        xb_w, xb_s = gather_packed(xo_w, xo_s, l2, "xb", "xb_w")
 
-        ca = []
-        for t in range(PACK):
-            if t == 0:
-                picked = keep.tile([P, O], F32, name="ca0", tag="tz0")
-            else:
-                picked = keep.tile([P, O], F32, name="ca%d" % t)
+        ca = [keep.tile([P, O], F32, name="ca%d" % t) for t in range(PACK)]
+        for h in range(2):
+            scalar_gather(ca[0][:, half(h)], a[0][:].indirect(half_list(l3, h)))
+        b = first_stage(xb_w, xb_s, E4M3, "b", nc.scalar.copy)
+        for t in range(1, PACK):
             for h in range(2):
-                scalar_gather(picked[:, half(h)], a[t][:].indirect(half_list(l3, h)))
-            ca.append(picked)
-
-        b = first_stage(xb_w, xb_s, E4M3, "b", nc.vector.tensor_copy)
+                vector_gather(ca[t][:, half(h)], a[t][:].indirect(half_list(l3, h)))
 
         sums = []
         for h in range(2):
@@ -183,7 +180,7 @@ def tile_list_secondhand_oneforboth_further_finalgate_kernel(
         bg = [[keep.tile([P, HALF], F32, name="bg%d_%d" % (h, t)) for t in range(PACK)] for h in range(2)]
         for h in range(2):
             for t in range(PACK):
-                gather = vector_gather if t < 2 else scalar_gather
+                gather = vector_gather if t == 0 else scalar_gather
                 gather(bg[h][t][:], b[t][:].indirect(half_list(l5, h)))
 
         diff = [keep.tile([P, PACK, HALF], F32, name="diff%d" % h) for h in range(2)]
@@ -192,7 +189,7 @@ def tile_list_secondhand_oneforboth_further_finalgate_kernel(
                 nc.vector.tensor_tensor(
                     out=diff[h][:, t, :], in0=ca[t][:].indirect(half_list(l4, h)), in1=bg[h][t][:], op=ALU.subtract
                 )
-        gate_rows(tz1, 1)
+        gate = keep.tile([P, 2, O], F32, name="gate", tag="b3")
 
         out_view = out.rearrange("(g p) o -> p g o", p=P)
         hid = []
@@ -204,6 +201,9 @@ def tile_list_secondhand_oneforboth_further_finalgate_kernel(
                 func=ACT.Abs,
             )
             hid.append(rounded)
+            if h == 0:
+                gate_rows(gate, tz0, 0)
+                gate_rows(gate, tz1, 1)
         for h in range(2):
             hq_w = keep.tile([P, HALF], U32, name="hq_w%d" % h, align_bytes=64)
             hq_s = keep.tile([P, HALF], U8, name="hq_s%d" % h, align_bytes=64)

@@ -95,6 +95,11 @@ def tile_list_secondhand_oneforboth_further_finalgate_kernel(
         wb_s = new_plane(wb_scales, "wb_s")
         load_quadrants(wb_s, wb_scales, range(4))
 
+        warm_in = keep.tile([P, 1], F32, name="warm_in")
+        warm_out = keep.tile([P, 1], F32, name="warm_out")
+        nc.vector.memset(warm_in[:], 0.0)
+        nc.scalar.activation(out=warm_out[:], in_=warm_in[:], func=ACT.Sigmoid)
+
         wp_w = keep.tile([P, 2 * R], U8, name="wp_w", align_bytes=64)
         wp_s = keep.tile([P, R], U8, name="wp_s", align_bytes=64)
         nc.vector.tensor_copy(

from contextlib import ExitStack

import concourse.mybir as mybir

F32 = mybir.dt.float32
BF16 = mybir.dt.bfloat16
I32 = mybir.dt.int32
U32 = mybir.dt.uint32
U16 = mybir.dt.uint16
U8 = mybir.dt.uint8
E4M3 = mybir.dt.float8_e4m3fn_x4
E5M2 = mybir.dt.float8_e5m2_x4
E2M1 = mybir.dt.float4_e2m1fn_x4
ACT = mybir.ActivationFunctionType
ALU = mybir.AluOpType

P = 128
PACK = 4
K, T, J, R, O, N, E = 512, 1024, 256, 512, 256, 256, 1024
HALF = O // 2
LIST_COLS = J // 16
HALF_COLS = LIST_COLS // 2

FLOPS = 2 * (2 * K * R * J + R * N * O + K * N * O)


def tile_list_secondhand_oneforboth_further_finalgate_kernel(
    tc, xt_words, xt_scales, xo_words, xo_scales, w_words, w_scales, wb_words, wb_scales, ws_words, ws_scales,
    tz, so, bo, offs, offs2, offs3, offs4, offs5, offs6, offs7, out,
):
    nc = tc.nc
    with ExitStack() as ctx:
        keep = ctx.enter_context(tc.tile_pool(name="keep", bufs=1))
        psum = ctx.enter_context(tc.psum_pool(name="psum", bufs=1))

        def load_list(src, name):
            lst = keep.tile([P, LIST_COLS], U16, name=name)
            nc.sync.dma_start(lst[:], src)
            return lst

        def load_fp8_words(queue, src, name):
            words = keep.tile([P, T], U32, name=name, align_bytes=64)
            queue.dma_start(words[:].bitcast(I32), src[0].rearrange("p c t -> p (c t)").bitcast(I32))
            return words

        def load_fp4_words(queue, src, name):
            words = keep.tile([P, src.shape[2]], U8, name=name, align_bytes=64)
            queue.dma_start(words[:].bitcast(I32), src[0].bitcast(I32))
            return words

        def new_plane(src, name):
            return keep.tile([P, src.shape[2]], U8, name=name, tag=name, align_bytes=64)

        def load_quadrants(plane, src, quadrants):
            rows = src[0].bitcast(I32)
            for q in quadrants:
                four = rows[4 * q : 4 * q + 4, :].unsqueeze(0).to_broadcast([8, 4, rows.shape[1]])
                nc.sync.dma_start(plane[32 * q : 32 * q + 32, :].bitcast(I32), four)

        def load_columns(src, name):
            cols = keep.tile([P, 2], F32, name=name)
            with nc.allow_non_contiguous_dma(reason="one value a partition"):
                nc.sync.dma_start(cols[:], src.rearrange("(h p) o -> p (h o)", p=P))
            return cols

        def load_gate_rows(h):
            rows = keep.tile([P, E], F32, name="tz%d" % h)
            nc.sync.dma_start(rows[:], tz[h * P : (h + 1) * P, :])
            return rows

        l1 = load_list(offs, "l1")
        l6 = load_list(offs6, "l6")
        xt_s = new_plane(xt_scales, "xt_s")
        load_quadrants(xt_s, xt_scales, range(4))
        w_w = load_fp4_words(nc.sync, w_words, "w_w")
        xt_w = load_fp8_words(nc.sync, xt_words, "xt_w")
        w_s = new_plane(w_scales, "w_s")
        load_quadrants(w_s, w_scales, range(4))
        xo_w = load_fp8_words(nc.sync, xo_words, "xo_w")
        l2 = load_list(offs2, "l2")
        xo_s = new_plane(xo_scales, "xo_s")
        load_quadrants(xo_s, xo_scales, range(4))
        l3 = load_list(offs3, "l3")
        l5 = load_list(offs5, "l5")
        l4 = load_list(offs4, "l4")
        l7 = load_list(offs7, "l7")
        tz0 = load_gate_rows(0)
        tz1 = load_gate_rows(1)
        slope = load_columns(so, "slope")
        offset = load_columns(bo, "offset")
        ws_w = load_fp4_words(nc.sync, ws_words, "ws_w")
        ws_s = new_plane(ws_scales, "ws_s")
        load_quadrants(ws_s, ws_scales, range(4))
        wb_w = load_fp4_words(nc.sync, wb_words, "wb_w")
        wb_s = new_plane(wb_scales, "wb_s")
        load_quadrants(wb_s, wb_scales, range(4))

        warm_in = keep.tile([P, 1], F32, name="warm_in")
        warm_out = keep.tile([P, 1], F32, name="warm_out")
        nc.vector.memset(warm_in[:], 0.0)
        nc.scalar.activation(out=warm_out[:], in_=warm_in[:], func=ACT.Sigmoid)

        wp_w = keep.tile([P, 2 * R], U8, name="wp_w", align_bytes=64)
        wp_s = keep.tile([P, R], U8, name="wp_s", align_bytes=64)
        nc.vector.tensor_copy(
            out=wp_w[:].bitcast(U16).rearrange("p (t m) -> p t m", t=PACK),
            in_=w_w[:].bitcast(U16).rearrange("p (m t) -> p t m", t=PACK),
        )
        nc.vector.tensor_copy(
            out=wp_s[:].rearrange("p (t m) -> p t m", t=PACK),
            in_=w_s[:].rearrange("p (m t) -> p t m", t=PACK),
        )

        def gather_packed(words, plane, lst, name, words_tag):
            got_w = keep.tile([P, J], U32, name=name + "_w", tag=words_tag, align_bytes=64)
            got_s = keep.tile([P, J], U8, name=name + "_s", align_bytes=64)
            nc.vector.tensor_copy(out=got_s[:], in_=plane[:].indirect(lst[:]))
            nc.vector.tensor_copy(out=got_w[:], in_=words[:].indirect(lst[:]))
            return got_w, got_s

        def first_stage(got_w, got_s, fmt, name, evacuate):
            res = []
            for t in range(PACK):
                acc = psum.tile([P, J], F32, name="acc_%s%d" % (name, t), tag="bank_%s%d" % (name, t))
                nc.tensor.matmul_mx(
                    out=acc[:],
                    lhsT=wp_w[:, 2 * P * t : 2 * P * (t + 1)].bitcast(E2M1),
                    lhsT_scale=wp_s[:, P * t : P * (t + 1)],
                    rhs=got_w[:].bitcast(fmt),
                    rhs_scale=got_s[:],
                    start=True,
                    stop=True,
                )
                rows = keep.tile([P, J], F32, name="%s%d" % (name, t), tag="%s%d" % (name, t))
                evacuate(out=rows[:], in_=acc[:])
                res.append(rows)
            return res

        def half_list(lst, h):
            return lst[:, h * HALF_COLS : (h + 1) * HALF_COLS]

        def half(h):
            return slice(h * HALF, (h + 1) * HALF)

        def scalar_gather(dst, window):
            nc.scalar.activation(out=dst, in_=window, func=ACT.Copy)

        def vector_gather(dst, window):
            nc.vector.tensor_copy(out=dst, in_=window)

        def gate_rows(gate, rows, h):
            nc.scalar.activation(
                out=gate[:, h, :], in_=rows[:].indirect(l7[:]), func=ACT.Sigmoid,
                bias=offset[:, h : h + 1], scale=slope[:, h : h + 1],
            )

        xa_w, xa_s = gather_packed(xt_w, xt_s, l1, "xa", "xa_w")
        a = first_stage(xa_w, xa_s, E5M2, "a", nc.scalar.copy)
        xs_w, xs_s = gather_packed(xt_w, xt_s, l6, "xs", "w_s")
        xb_w, xb_s = gather_packed(xo_w, xo_s, l2, "xb", "xb_w")

        ca = [keep.tile([P, O], F32, name="ca%d" % t) for t in range(PACK)]
        for h in range(2):
            scalar_gather(ca[0][:, half(h)], a[0][:].indirect(half_list(l3, h)))
        b = first_stage(xb_w, xb_s, E4M3, "b", nc.scalar.copy)
        for t in range(1, PACK):
            for h in range(2):
                vector_gather(ca[t][:, half(h)], a[t][:].indirect(half_list(l3, h)))

        sums = []
        for h in range(2):
            acc = psum.tile([P, 2, HALF], F32, name="sum%d" % h, tag="bank_a%d" % h)
            for g in range(2):
                nc.tensor.matmul_mx(
                    out=acc[:, g, :],
                    lhsT=ws_w[:, 2 * P * g : 2 * P * (g + 1)].bitcast(E2M1),
                    lhsT_scale=ws_s[:, P * g : P * (g + 1)],
                    rhs=xs_w[:, half(h)].bitcast(E5M2),
                    rhs_scale=xs_s[:, half(h)],
                    start=(g == 0),
                    stop=False,
                )
            sums.append(acc)

        bg = [[keep.tile([P, HALF], F32, name="bg%d_%d" % (h, t)) for t in range(PACK)] for h in range(2)]
        for h in range(2):
            for t in range(PACK):
                gather = vector_gather if t == 0 else scalar_gather
                gather(bg[h][t][:], b[t][:].indirect(half_list(l5, h)))

        diff = [keep.tile([P, PACK, HALF], F32, name="diff%d" % h) for h in range(2)]
        for h in range(2):
            for t in range(PACK):
                nc.vector.tensor_tensor(
                    out=diff[h][:, t, :], in0=ca[t][:].indirect(half_list(l4, h)), in1=bg[h][t][:], op=ALU.subtract
                )
        gate = keep.tile([P, 2, O], F32, name="gate", tag="b3")

        out_view = out.rearrange("(g p) o -> p g o", p=P)
        hid = []
        for h in range(2):
            rounded = keep.tile([P, HALF * PACK], BF16, name="hid%d" % h, align_bytes=64)
            nc.scalar.activation(
                out=rounded[:].rearrange("p (c i t) -> p c t i", i=4, t=PACK),
                in_=diff[h][:].rearrange("p t (c i) -> p c t i", i=4),
                func=ACT.Abs,
            )
            hid.append(rounded)
            if h == 0:
                gate_rows(gate, tz0, 0)
                gate_rows(gate, tz1, 1)
        for h in range(2):
            hq_w = keep.tile([P, HALF], U32, name="hq_w%d" % h, align_bytes=64)
            hq_s = keep.tile([P, HALF], U8, name="hq_s%d" % h, align_bytes=64)
            nc.vector.quantize_mx(out=hq_w[:].bitcast(E4M3), scales=hq_s[:], in_=hid[h][:])
            for g in range(2):
                nc.tensor.matmul_mx(
                    out=sums[h][:, g, :],
                    lhsT=wb_w[:, 2 * P * g : 2 * P * (g + 1)].bitcast(E2M1),
                    lhsT_scale=wb_s[:, P * g : P * (g + 1)],
                    rhs=hq_w[:].bitcast(E4M3),
                    rhs_scale=hq_s[:],
                    start=False,
                    stop=(g == 1),
                )
            y = keep.tile([P, 2, HALF], F32, name="y%d" % h)
            nc.vector.tensor_tensor(out=y[:], in0=sums[h][:], in1=gate[:, :, half(h)], op=ALU.mult)
            nc.sync.dma_start(out_view[:, :, half(h)], y[:])
